import numpy as np
import ml_dtypes


def mxq(x, axis, fmt="e4m3"):
    dtype, down = {"e4m3": (ml_dtypes.float8_e4m3fn, 7), "e5m2": (ml_dtypes.float8_e5m2, 14)}[fmt]
    v = np.moveaxis(np.asarray(x, np.float32).astype(ml_dtypes.bfloat16).astype(np.float64), axis, -1)
    blocks = v.reshape(v.shape[:-1] + (-1, 32))
    amax = np.abs(blocks).max(-1, keepdims=True)
    byte = np.maximum(np.where(amax > 0, np.frexp(amax)[1] - 1 + 127, 0) - down, 1)
    scale = np.exp2(byte - 127.0)
    codes = (blocks / scale).astype(np.float32).astype(dtype).astype(np.float64)
    return np.moveaxis((codes * scale).reshape(v.shape), -1, axis)


WIDE = False


def mx_kscale(k):
    if not WIDE:
        return np.ones(k)
    levels = np.array([10, -10, 5, -5, 0])
    if k % 512:
        return np.exp2(np.random.permutation(np.resize(levels, k // 32))).repeat(32)
    a = np.empty((k // 512, 16))
    for p in range(k // 512):
        a[p, :8] = np.random.permutation(np.resize(levels, 8))
        for g in range(8):
            far = levels[np.abs(levels - a[p, g]) >= 10]
            a[p, g + 8] = far[np.random.randint(len(far))]
    return np.exp2(a.ravel()).repeat(32)


def f64(x):
    return np.asarray(x).astype(np.float64)


def striped(idx):
    return np.tile(idx.reshape(-1, 16).T, (8, 1)).astype(np.uint16)


def unstriped(offs):
    return offs[:16].T.reshape(-1).astype(np.int64)


def pack_weight(w):
    k, n = w.shape
    w = f64(np.asarray(w, np.float32).astype(ml_dtypes.bfloat16)).reshape(k // 32, 32, n)
    amax = np.abs(w).max(1)
    byte = np.clip(np.where(amax > 0, np.frexp(amax)[1] - 1 + 127 - 7, 1), 1, 254)
    scaled = (w * np.exp2(127.0 - byte)[:, None, :]).reshape(k, n).astype(np.float32)
    words = np.ascontiguousarray(scaled.reshape(k // 512, 128, 4, n).transpose(0, 1, 3, 2)).astype(ml_dtypes.float8_e4m3fn).view(np.uint8)
    return words, np.ascontiguousarray(byte.astype(np.uint8).reshape(k // 512, 16, n))


def unpack_weight(words, scales):
    g, p, n, _ = words.shape
    vals = np.ascontiguousarray(words).view(ml_dtypes.float8_e4m3fn).astype(np.float64) * np.repeat(np.exp2(scales.astype(np.float64) - 127.0), 8, axis=1)[..., None]
    return vals.transpose(0, 1, 3, 2).reshape(g * 512, n)


def sigmoid(v):
    return 1.0 / (1.0 + np.exp(-np.maximum(v, -700.0)))


K, T, S, N, H, W, G = 512, 2048, 512, 128, 512, 2048, 1024


def setup_inputs():
    n = np.random.standard_normal
    s = mx_kscale(K)[:, None]
    u = mx_kscale(H)
    packed_xT = pack_weight(n((K, T)) * s)
    packed_eT = pack_weight(n((K, W)) * s)
    packed_dT = pack_weight(n((K, G)) * s)
    return {
        "x_words": packed_xT[0],
        "x_scales": packed_xT[1],
        "w1": (n((K, H)) / np.sqrt(K) / s).astype(np.float32),
        "e_words": packed_eT[0],
        "e_scales": packed_eT[1],
        "w2": (n((K, H)) / np.sqrt(K) / s).astype(np.float32),
        "d_words": packed_dT[0],
        "d_scales": packed_dT[1],
        "w3": (n((K, H)) / np.sqrt(K) / s).astype(np.float32),
        "unit": (np.random.uniform(0.6, 1.4, (H, 1)) * u[:, None]).astype(np.float32),
        "w4": (n((H, N)) / np.sqrt(H) / u[:, None]).astype(np.float32),
        "offs": striped(np.random.permutation(T)[:S]),
        "ovl": striped(np.random.permutation(W)[:S]),
        "lab": striped(np.random.permutation(G)[:S]),
        "sh1": striped(np.random.permutation(S)),
        "px": striped(np.random.permutation(S)),
    }


def reference(x_words, x_scales, w1, e_words, e_scales, w2, d_words, d_scales, w3, unit, w4, offs, ovl, lab, sh1, px):
    d_lab = unpack_weight(d_words, d_scales)[:, unstriped(lab)]
    yd = mxq(f64(w3), 0, "e4m3").T @ d_lab
    alp = sigmoid(2.0 * yd)
    xq = unpack_weight(x_words, x_scales)[:, unstriped(offs)]
    y = mxq(f64(w1), 0, "e4m3").T @ xq
    e_ovl = unpack_weight(e_words, e_scales)[:, unstriped(ovl)]
    ye = mxq(f64(w2), 0, "e4m3").T @ e_ovl
    es1 = ye[:, unstriped(sh1)]
    cmp1 = np.maximum(y, 0.8 * es1)
    cov = alp * yd + (-1.0 * alp + 1.0) * cmp1
    zp = cov[:, unstriped(px)]
    hid = f64(unit) * (zp - (0.3 * y))
    return mxq(f64(w4), 0, "e4m3").T @ mxq(hid, 0, "e4m3")

from contextlib import ExitStack

import concourse.mybir as mybir

K, S, N, H = 512, 512, 128, 512
FLOPS = 2 * K * H * S * 3 + 2 * H * N * S

F32 = mybir.dt.float32
BF16 = mybir.dt.bfloat16
I32 = mybir.dt.int32
U32 = mybir.dt.uint32
U16 = mybir.dt.uint16
U8 = mybir.dt.uint8
FP8X4 = mybir.dt.float8_e4m3fn_x4
ALU = mybir.AluOpType
ACT = mybir.ActivationFunctionType

P = 128
PACK = 4
HALF = S // 2
LIST_COLS = S // 16
VECTOR_SHARE = 80


def tile_picked_ymapovl_diff_p_kernel(
    tc, x_words, x_scales, w1, e_words, e_scales, w2, d_words, d_scales, w3, unit, w4, offs, ovl, lab, sh1, px, out
):
    nc = tc.nc
    with ExitStack() as ctx:
        keep = ctx.enter_context(tc.tile_pool(name="keep", bufs=1))
        psum = ctx.enter_context(tc.psum_pool(name="psum", bufs=1))

        def load_list(name, src):
            t = keep.tile([P, LIST_COLS], U16, name=name)
            nc.sync.dma_start(t[:], src)
            return t

        def load_weight(name, w):
            raw = keep.tile([P, PACK * w.shape[1]], F32, name=name)
            nc.sync.dma_start(raw[:], w.rearrange("(p j) c -> p (j c)", j=PACK))
            return raw

        def load_words(name, words):
            t = keep.tile([P, words.shape[2]], U32, name=name)
            nc.sync.dma_start(t[:].bitcast(I32), words[0].rearrange("p n r -> p (n r)").bitcast(I32))
            return t

        def load_scales(name, scales, queue):
            t = keep.tile([P, scales.shape[2]], U8, name=name)
            nc.vector.memset(t[:].bitcast(I32), 0)
            for q in range(4):
                queue.dma_start(t[32 * q : 32 * q + 4, :].bitcast(I32), scales[0, 4 * q : 4 * q + 4, :].bitcast(I32))
            return t

        def pick(name, table, offsets, dtype):
            t = keep.tile([P, S], dtype, name=name, align_bytes=64)
            nc.vector.tensor_copy(t[:], table[:].indirect(offsets[:]))
            return t

        def deal(raw, grouped, m0, m1, copy):
            src = raw[:].rearrange("p (j m t) -> p m j t", j=PACK, t=PACK)
            dst = grouped[:].rearrange("p (t m j) -> p m j t", j=PACK, t=PACK)
            copy(dst[:, m0:m1], src[:, m0:m1])

        def quantise(name, grouped):
            width = grouped.shape[1] // PACK
            codes = keep.tile([P, width], U32, name=name + "_codes", align_bytes=64)
            scales = keep.tile([P, width], U8, name=name + "_scales", align_bytes=64)
            nc.vector.quantize_mx(out=codes[:].bitcast(FP8X4), scales=scales[:], in_=grouped[:])
            return codes, scales

        def product(acc, w_codes, w_scales, codes, scales):
            nc.tensor.matmul_mx(
                out=acc, lhsT=w_codes.bitcast(FP8X4), lhsT_scale=w_scales,
                rhs=codes.bitcast(FP8X4), rhs_scale=scales, start=True, stop=True,
            )

        def interleave(dst, src, copy):
            copy(
                dst.rearrange("p (c i t) -> p c t i", i=4, t=PACK),
                src.rearrange("p (t c i) -> p c t i", i=4, t=PACK),
            )

        u = keep.tile([P, PACK], F32, name="u")
        nc.scalar.dma_start(u[:], unit.rearrange("(p t) o -> p (t o)", t=PACK))
        d_table = load_words("d_table", d_words)
        lab_t = load_list("lab_t", lab)
        d_plane = load_scales("d_plane", d_scales, nc.sync)
        w3_raw = load_weight("w3_raw", w3)
        e_plane = load_scales("e_plane", e_scales, nc.sync)
        w2_raw = load_weight("w2_raw", w2)
        ovl_t = load_list("ovl_t", ovl)
        e_table = load_words("e_table", e_words)
        offs_t = load_list("offs_t", offs)
        x_plane = load_scales("x_plane", x_scales, nc.sync)
        w1_raw = load_weight("w1_raw", w1)
        sh1_t = load_list("sh1_t", sh1)
        x_table = load_words("x_table", x_words)
        px_t = load_list("px_t", px)
        w4_raw = load_weight("w4_raw", w4)

        sign = keep.tile([P, PACK], F32, name="sign")
        step = keep.tile([P, PACK], F32, name="step")
        half_u = keep.tile([P, PACK], F32, name="half_u")
        half_abs = keep.tile([P, PACK], F32, name="half_abs")
        overlay_abs = keep.tile([P, PACK], F32, name="overlay_abs")
        base_u = keep.tile([P, PACK], F32, name="base_u")
        nc.vector.tensor_scalar(step[:], u[:], 0.0, 2.0, ALU.is_ge, ALU.mult)
        nc.vector.tensor_scalar(half_u[:], u[:], 0.5, None, ALU.mult)
        nc.vector.tensor_scalar(sign[:], step[:], -1.0, None, ALU.add)
        nc.vector.tensor_scalar(base_u[:], u[:], -0.3, None, ALU.mult)
        nc.vector.tensor_tensor(half_abs[:], half_u[:], sign[:], ALU.mult)
        nc.vector.tensor_scalar(overlay_abs[:], half_abs[:], 0.8, None, ALU.mult)

        tiles = range(PACK)
        cols = [slice(t * P, (t + 1) * P) for t in tiles]
        halves = [slice(0, HALF), slice(HALF, S)]
        list_halves = [slice(0, LIST_COLS // 2), slice(LIST_COLS // 2, LIST_COLS)]

        d_codes = pick("d_codes", d_table, lab_t, U32)
        d_bytes = pick("d_bytes", d_plane, lab_t, U8)
        w3_grouped = keep.tile([P, PACK * H], BF16, name="w3_grouped", align_bytes=64)
        deal(w3_raw, w3_grouped, 0, VECTOR_SHARE, nc.vector.tensor_copy)
        deal(w3_raw, w3_grouped, VECTOR_SHARE, P, nc.scalar.copy)
        w3_codes, w3_scales = quantise("w3", w3_grouped)
        silu, tanh = [], []
        for t in tiles:
            yd = psum.tile([P, S], F32, name="bank_a%d" % t)
            product(yd[:], w3_codes[:, cols[t]], w3_scales[:, cols[t]], d_codes[:], d_bytes[:])
            silu.append(keep.tile([P, S], F32, name="silu%d" % t))
            tanh.append(keep.tile([P, S], F32, name="tanh%d" % t))
            nc.scalar.activation(silu[t][:], yd[:], ACT.Silu, scale=2.0)
            nc.scalar.activation(tanh[t][:], yd[:], ACT.Tanh, scale=sign[:, t : t + 1])

        e_bytes = pick("e_bytes", e_plane, ovl_t, U8)
        w2_grouped = keep.tile([P, PACK * H], BF16, name="w2_grouped", align_bytes=64)
        deal(w2_raw, w2_grouped, 0, P, nc.vector.tensor_copy)
        w2_codes, w2_scales = quantise("w2", w2_grouped)
        e_codes = pick("e_codes", e_table, ovl_t, U32)
        shifted = []
        for t in tiles:
            ye = psum.tile([P, S], F32, name="bank_b%d" % t)
            product(ye[:], w2_codes[:, cols[t]], w2_scales[:, cols[t]], e_codes[:], e_bytes[:])
            overlay = keep.tile([P, S], F32, name="overlay%d" % t)
            nc.scalar.activation(overlay[:], ye[:], ACT.Copy, scale=overlay_abs[:, t : t + 1])
            shifted.append(keep.tile([P, S], F32, name="shifted%d" % t))
            for h in range(2):
                nc.scalar.activation(shifted[t][:, halves[h]], overlay[:].indirect(sh1_t[:, list_halves[h]]), ACT.Copy)

        w1_grouped = keep.tile([P, PACK * H], BF16, name="w1_grouped", align_bytes=64)
        x_bytes = pick("x_bytes", x_plane, offs_t, U8)
        deal(w1_raw, w1_grouped, 0, P, nc.vector.tensor_copy)
        w1_codes, w1_scales = quantise("w1", w1_grouped)
        x_codes = pick("x_codes", x_table, offs_t, U32)
        y = []
        for t in tiles:
            y.append(psum.tile([P, S], F32, name="bank_a%d" % t))
            product(y[t][:], w1_codes[:, cols[t]], w1_scales[:, cols[t]], x_codes[:], x_bytes[:])

        w4_grouped = keep.tile([P, PACK * N], BF16, name="w4_grouped", align_bytes=64)
        interleave(w4_grouped[:], w4_raw[:], nc.scalar.copy)

        top = [keep.tile([P, S], F32, name="top%d" % t) for t in tiles]
        under = [keep.tile([P, S], F32, name="under%d" % t) for t in tiles]
        cover = [keep.tile([P, S], F32, name="cover%d" % t) for t in tiles]
        placed = [keep.tile([P, S], F32, name="placed%d" % t) for t in tiles]

        def take_max(t):
            nc.vector.scalar_tensor_tensor(top[t][:], y[t][:], half_abs[:, t : t + 1], shifted[t][:], ALU.mult, ALU.max)

        def weigh(t):
            nc.vector.scalar_tensor_tensor(under[t][:], tanh[t][:], sign[:, t : t + 1], top[t][:], ALU.subtract, ALU.mult)

        def blend(t):
            nc.vector.scalar_tensor_tensor(cover[t][:], silu[t][:], half_u[:, t : t + 1], under[t][:], ALU.mult, ALU.subtract)
            for h in range(2):
                nc.scalar.activation(placed[t][:, halves[h]], cover[t][:].indirect(px_t[:, list_halves[h]]), ACT.Copy)

        for s in range(PACK + 2):
            if s < PACK:
                take_max(s)
            if s >= 2:
                blend(s - 2)
            if 1 <= s <= PACK:
                weigh(s - 1)

        w4_codes, w4_scales = quantise("w4", w4_grouped)
        hid = [keep.tile([P, PACK * HALF], BF16, name="hid%d" % h) for h in range(2)]
        for t in tiles:
            for h in range(2):
                nc.vector.scalar_tensor_tensor(
                    hid[h][:, t * HALF : (t + 1) * HALF], y[t][:, halves[h]], base_u[:, t : t + 1],
                    placed[t][:, halves[h]], ALU.mult, ALU.add,
                )
        for h, copy in ((0, nc.scalar.copy), (1, nc.vector.tensor_copy)):
            hid_grouped = keep.tile([P, PACK * HALF], BF16, name="hid_grouped%d" % h, align_bytes=64)
            interleave(hid_grouped[:], hid[h][:], copy)
            hid_codes, hid_scales = quantise("hid%d" % h, hid_grouped)
            acc = psum.tile([P, HALF], F32, name="bank_b%d" % h)
            product(acc[:], w4_codes[:], w4_scales[:], hid_codes[:], hid_scales[:])
            result = keep.tile([P, HALF], F32, name="result%d" % h)
            copy(result[:], acc[:])
            nc.sync.dma_start(out[:, halves[h]], result[:])
